import numpy as np
import ml_dtypes


def mxq(x, axis, fmt="e4m3"):
    dtype, down = {"e4m3": (ml_dtypes.float8_e4m3fn, 7), "e5m2": (ml_dtypes.float8_e5m2, 14)}[fmt]
    v = np.moveaxis(np.asarray(x, np.float32).astype(ml_dtypes.bfloat16).astype(np.float64), axis, -1)
    blocks = v.reshape(v.shape[:-1] + (-1, 32))
    amax = np.abs(blocks).max(-1, keepdims=True)
    byte = np.maximum(np.where(amax > 0, np.frexp(amax)[1] - 1 + 127, 0) - down, 1)
    scale = np.exp2(byte - 127.0)
    codes = (blocks / scale).astype(np.float32).astype(dtype).astype(np.float64)
    return np.moveaxis((codes * scale).reshape(v.shape), -1, axis)


WIDE = False


def mx_kscale(k):
    if not WIDE:
        return np.ones(k)
    levels = np.array([24, -24, 12, -12, 0])
    if k % 512:
        return np.exp2(np.random.permutation(np.resize(levels, k // 32))).repeat(32)
    a = np.empty((k // 512, 16))
    for p in range(k // 512):
        a[p, :8] = np.random.permutation(np.resize(levels, 8))
        for g in range(8):
            far = levels[np.abs(levels - a[p, g]) >= 10]
            a[p, g + 8] = far[np.random.randint(len(far))]
    return np.exp2(a.ravel()).repeat(32)


def f64(x):
    return np.asarray(x).astype(np.float64)


def striped(idx):
    return np.tile(idx.reshape(-1, 16).T, (8, 1)).astype(np.uint16)


def unstriped(offs):
    return offs[:16].T.reshape(-1).astype(np.int64)


E2M1 = np.array([0.0, 0.5, 1.0, 1.5, 2.0, 3.0, 4.0, 6.0, -0.0, -0.5, -1.0, -1.5, -2.0, -3.0, -4.0, -6.0])


def pack_weight(w, fmt):
    k, n = w.shape
    w = f64(np.asarray(w, np.float32).astype(ml_dtypes.bfloat16)).reshape(k // 32, 32, n)
    amax = np.abs(w).max(1)
    if fmt == "e4m3":
        byte = np.frexp(amax)[1] - 1 + 127 - 7
    else:
        mant, ex = np.frexp(amax / 6.0)
        byte = np.where(mant > 0.5, ex, ex - 1) + 127
    byte = np.clip(np.where(amax > 0, byte, 1), 1, 254)
    scaled = (w * np.exp2(127.0 - byte)[:, None, :]).reshape(k, n).astype(np.float32)
    by_word = np.ascontiguousarray(scaled.reshape(k // 512, 128, 4, n).transpose(0, 1, 3, 2))
    if fmt == "e4m3":
        words = by_word.astype(ml_dtypes.float8_e4m3fn).view(np.uint8)
    else:
        c = by_word.astype(ml_dtypes.float4_e2m1fn).view(np.uint8) & 0xF
        words = (c[..., 0::2] | (c[..., 1::2] << 4)).reshape(k // 512, 128, 2 * n)
    return np.ascontiguousarray(words), np.ascontiguousarray(byte.astype(np.uint8).reshape(k // 512, 16, n))


def unpack_weight(words, scales, fmt):
    g, _, n = scales.shape
    words = np.ascontiguousarray(words).reshape(g, 128, n, -1)
    if fmt == "e4m3":
        vals = words.view(ml_dtypes.float8_e4m3fn).astype(np.float64)
    else:
        nib = np.empty((g, 128, n, 4), np.uint8)
        nib[..., 0::2] = words & 0xF
        nib[..., 1::2] = words >> 4
        vals = E2M1[nib]
    vals = vals * np.repeat(np.exp2(scales.astype(np.float64) - 127.0), 8, axis=1)[..., None]
    return vals.transpose(0, 1, 3, 2).reshape(g * 512, n)


K, N, T, J = 512, 512, 4096, 1024


def setup_inputs():
    n = np.random.standard_normal
    s = mx_kscale(K)[:, None]
    p_tab = pack_weight(n((K, T)) * s, "e4m3")
    p_tab2 = pack_weight(n((K, T)) * s, "e4m3")
    p_wr4 = pack_weight(n((K, N)) / np.sqrt(2 * K) / s, "e2m1")
    return {
        "tab_words": p_tab[0],
        "tab_scales": p_tab[1],
        "tab2_words": p_tab2[0],
        "tab2_scales": p_tab2[1],
        "wr4_words": p_wr4[0],
        "wr4_scales": p_wr4[1],
        "wrd": (0.4 * (n((K, N)) / np.sqrt(2 * K) / s)).astype(np.float32),
        "wi": (n((K, N)) / np.sqrt(2 * K) / s).astype(np.float32),
        "br": (0.3 * n(N)).astype(np.float32),
        "bi": (0.3 * n(N)).astype(np.float32),
        "offs": striped(np.random.permutation(T)[:J]),
    }


def reference(tab_words, tab_scales, tab2_words, tab2_scales, wr4_words, wr4_scales, wrd, wi, br, bi, offs):
    idx = unstriped(offs)
    tab_ = unpack_weight(tab_words, tab_scales, "e4m3")[:, idx]
    tab2_ = unpack_weight(tab2_words, tab2_scales, "e4m3")[:, idx]
    wr4_ = unpack_weight(wr4_words, wr4_scales, "e2m1")
    wrd_ = mxq(f64(wrd), 0, "e4m3")
    wi_ = mxq(f64(wi), 0, "e4m3")
    rr = wr4_.T @ tab_ + wrd_.T @ tab_
    ii = wi_.T @ tab2_
    zr = rr - ii
    ri = wr4_.T @ tab2_ + wrd_.T @ tab2_ + wi_.T @ tab_
    zi = ri
    return zr + f64(br)[:, None], zi + f64(bi)[:, None]

@@ -1,0 +1,203 @@
+from contextlib import ExitStack
+
+import concourse.mybir as mybir
+from concourse.masks import make_identity
+
+K, N, T, J = 512, 512, 4096, 1024
+FLOPS = 6 * 2 * K * N * J
+
+F32 = mybir.dt.float32
+BF16 = mybir.dt.bfloat16
+I32 = mybir.dt.int32
+U32 = mybir.dt.uint32
+U16 = mybir.dt.uint16
+U8 = mybir.dt.uint8
+FP8X4 = mybir.dt.float8_e4m3fn_x4
+FP4X4 = mybir.dt.float4_e2m1fn_x4
+ADD = mybir.AluOpType.add
+MULT = mybir.AluOpType.mult
+IDENTITY = mybir.ActivationFunctionType.Identity
+
+P = 128
+PACK = 4
+M = 128
+JH = 512
+NH = 256
+
+
+def tile_list_cpxtab_dl_bias_kernel(
+    tc, tab_words, tab_scales, tab2_words, tab2_scales, wr4_words, wr4_scales, wrd, wi, br, bi, offs, out_0, out_1
+):
+    nc = tc.nc
+    with ExitStack() as ctx:
+        held = ctx.enter_context(tc.tile_pool(name="held", bufs=1))
+        raws = ctx.enter_context(tc.tile_pool(name="raws", bufs=2))
+        psum = ctx.enter_context(tc.psum_pool(name="psum", bufs=8))
+
+        def words_ap(words):
+            return words[0].rearrange("p t i -> p (t i)").bitcast(I32)
+
+        offsets = held.tile([P, J // 16], U16, name="offsets")
+        nc.sync.dma_start(offsets[:], offs)
+        bias_rows = held.tile([P, P], F32, name="bias_rows", tag="v2_slot")
+        nc.gpsimd.memset(bias_rows[:], 0.0)
+        nc.scalar.dma_start(bias_rows[0:4, :], br.rearrange("(c p) -> c p", p=P))
+        nc.scalar.dma_start(bias_rows[4:8, :], bi.rearrange("(c p) -> c p", p=P))
+        identity = held.tile([P, P], F32, name="identity", tag="v_slot")
+        make_identity(nc, identity[:])
+
+        def load_scale_window(name, scales):
+            window = held.tile([P, T // 4], I32, name=name)
+            nc.vector.memset(window[:], 0)
+            nc.scalar.dma_start(window[0:P:8, :], scales[0].bitcast(I32))
+            return window
+
+        s2_window = load_scale_window("s2_window", tab2_scales)
+        s_window = load_scale_window("s_window", tab_scales)
+
+        w4_codes = held.tile([P, 2 * N], U8, name="w4_codes", align_bytes=64)
+        nc.sync.dma_start(w4_codes[:].bitcast(I32), wr4_words[0].bitcast(I32))
+
+        def load_raw(name, w, c0, width):
+            raw = raws.tile([P, PACK, width], F32, name=name, tag="raw")
+            nc.sync.dma_start(raw[:], w.rearrange("(p j) n -> p j n", j=PACK)[:, :, c0 : c0 + width])
+            return raw
+
+        wrd_raw = load_raw("wrd_raw", wrd, 0, N)
+        wi_raw_a = load_raw("wi_raw_a", wi, 0, NH)
+
+        w4_scales = held.tile([P, N], U8, name="w4_scales", align_bytes=64)
+        nc.gpsimd.memset(w4_scales[:], 0)
+        for q in range(4):
+            nc.gpsimd.dma_start(
+                w4_scales[32 * q : 32 * q + 4, :].bitcast(I32), wr4_scales[0, 4 * q : 4 * q + 4, :].bitcast(I32)
+            )
+        bias_bank = psum.tile([P, JH], F32, name="bias_bank", tag="bank")
+        nc.tensor.transpose(bias_bank[:, 0:P], bias_rows[:], identity[:])
+        bias = held.tile([P, 8], F32, name="bias")
+        nc.scalar.activation(bias[:], bias_bank[:, 0:8], IDENTITY)
+        v2_window = held.tile([P, T], I32, name="v2_window", tag="v2_slot")
+        nc.sync.dma_start(v2_window[:], words_ap(tab2_words))
+        v_window = held.tile([P, T], I32, name="v_window", tag="v_slot")
+        nc.sync.dma_start(v_window[:], words_ap(tab_words))
+
+        def gather_scales(name, window):
+            picked = held.tile([P, J], U8, name=name + "_picked", align_bytes=64)
+            nc.vector.tensor_copy(picked[:], window[:].bitcast(U8).indirect(offsets[:]))
+            plane = held.tile([P, J], U8, name=name + "_plane", align_bytes=64)
+            nc.vector.tensor_copy(plane[:].bitcast(I32), picked[:].bitcast(I32))
+            for r in range(1, 4):
+                nc.scalar.dma_start(plane[r:P:32, :].bitcast(I32), picked[8 * r : P : 32, :].bitcast(I32))
+            return plane
+
+        def gather_words(name, window, h):
+            picked = held.tile([P, JH], U32, name=name + "_%d" % h, align_bytes=64)
+            cols = JH // 16
+            nc.vector.tensor_copy(picked[:], window[:].bitcast(U32).indirect(offsets[:, h * cols : (h + 1) * cols]))
+            return picked
+
+        s2_plane = gather_scales("s2", s2_window)
+        s_plane = gather_scales("s", s_window)
+        v2_codes = [gather_words("v2_codes", v2_window, h) for h in range(2)]
+
+        def new_weight(name):
+            return (
+                held.tile([P, N], U32, name=name + "_codes", align_bytes=64),
+                held.tile([P, N], U8, name=name + "_scales", align_bytes=64),
+            )
+
+        wrd_q = new_weight("wrd")
+        wi_q = new_weight("wi")
+        neg_q = new_weight("neg_wi")
+
+        def quantize(weight, c0, grouped):
+            codes, scales = weight
+            nc.vector.quantize_mx(
+                out=codes[:, c0 : c0 + NH].bitcast(FP8X4),
+                scales=scales[:, c0 : c0 + NH],
+                in_=grouped[:].rearrange("p n j -> p (n j)"),
+            )
+
+        def interleave(name, raw_cols, on_scalar):
+            grouped = held.tile([P, NH, PACK], BF16, name=name, align_bytes=64)
+            if on_scalar:
+                nc.scalar.copy(grouped[:], raw_cols.rearrange("p j n -> p n j"))
+            else:
+                nc.vector.tensor_copy(grouped[:], raw_cols.rearrange("p j n -> p n j"))
+            return grouped
+
+        def negate(name, grouped):
+            negated = held.tile([P, NH, PACK], BF16, name=name, align_bytes=64)
+            nc.vector.tensor_scalar(negated[:], grouped[:], -1.0, None, MULT)
+            return negated
+
+        def mx_pass(bank, weight, n, codes, plane, h, start, stop):
+            if weight is None:
+                lhs = w4_codes[:, 2 * M * n : 2 * M * (n + 1)].bitcast(FP4X4)
+                lhs_scale = w4_scales[:, M * n : M * (n + 1)]
+            else:
+                lhs = weight[0][:, M * n : M * (n + 1)].bitcast(FP8X4)
+                lhs_scale = weight[1][:, M * n : M * (n + 1)]
+            nc.tensor.matmul_mx(
+                out=bank[:],
+                lhsT=lhs,
+                lhsT_scale=lhs_scale,
+                rhs=codes[h][:].bitcast(FP8X4),
+                rhs_scale=plane[:, JH * h : JH * (h + 1)],
+                start=start,
+                stop=stop,
+            )
+
+        zi_banks = {}
+        for h in range(2):
+            for n in range(4):
+                zi_banks[n, h] = psum.tile([P, JH], F32, name="zi_%d_%d" % (n, h), tag="bank")
+                mx_pass(zi_banks[n, h], None, n, v2_codes, s2_plane, h, True, False)
+        for a in range(2):
+            quantize(wrd_q, NH * a, interleave("wrd_g%d" % a, wrd_raw[:, :, NH * a : NH * (a + 1)], True))
+            for n in (2 * a, 2 * a + 1):
+                for h in range(2):
+                    mx_pass(zi_banks[n, h], wrd_q, n, v2_codes, s2_plane, h, False, False)
+        wi_raw_b = load_raw("wi_raw_b", wi, NH, NH)
+        wi_g = interleave("wi_g0", wi_raw_a[:], True)
+        neg_g = negate("neg_g0", wi_g)
+        quantize(wi_q, 0, wi_g)
+        quantize(neg_q, 0, neg_g)
+
+        v_codes = [gather_words("v_codes", v_window, h) for h in range(2)]
+        wi_g = interleave("wi_g1", wi_raw_b[:], False)
+        neg_g = negate("neg_g1", wi_g)
+        quantize(wi_q, NH, wi_g)
+        quantize(neg_q, NH, neg_g)
+
+        results = {}
+        for part in range(2):
+            for n in range(4):
+                results[part, n] = held.tile([P, J], F32, name="result_%d_%d" % (part, n))
+        outs = (out_0, out_1)
+
+        order = [(1, 0, 0), (1, 1, 0), (0, 0, 0), (1, 0, 1), (1, 1, 1), (0, 0, 1)]
+        order += [(1, n, h) for n in (2, 3) for h in range(2)]
+        order += [(0, n, h) for n in (1, 2, 3) for h in range(2)]
+        paired = [(1, 2), (1, 3), (0, 1), (0, 2)]
+        for i, (part, n, h) in enumerate(order):
+            if part == 1:
+                bank = zi_banks[n, h]
+                mx_pass(bank, wi_q, n, v_codes, s_plane, h, False, True)
+            else:
+                bank = psum.tile([P, JH], F32, name="zr_%d_%d" % (n, h), tag="bank")
+                mx_pass(bank, neg_q, n, v2_codes, s2_plane, h, True, False)
+                mx_pass(bank, None, n, v_codes, s_plane, h, False, False)
+                mx_pass(bank, wrd_q, n, v_codes, s_plane, h, False, True)
+            cols = slice(JH * h, JH * (h + 1))
+            result = results[part, n]
+            column = bias[:, 4 * part + n : 4 * part + n + 1]
+            if i >= 5 and i % 2 == 1:
+                nc.vector.tensor_scalar(result[:, cols], bank[:], column, None, ADD)
+            else:
+                nc.scalar.activation(result[:, cols], bank[:], IDENTITY, bias=column)
+            rows = slice(M * n, M * (n + 1))
+            if (part, n) not in paired:
+                nc.sync.dma_start(outs[part][rows, cols], result[:, cols])
+            elif h == 1:
+                nc.sync.dma_start(outs[part][rows, :], result[:])

@@ -31,63 +31,60 @@ def tile_list_cpxtab_dl_bias_kernel(
     nc = tc.nc
     with ExitStack() as ctx:
         held = ctx.enter_context(tc.tile_pool(name="held", bufs=1))
-        raws = ctx.enter_context(tc.tile_pool(name="raws", bufs=2))
         psum = ctx.enter_context(tc.psum_pool(name="psum", bufs=8))
 
         def words_ap(words):
             return words[0].rearrange("p t i -> p (t i)").bitcast(I32)
 
+        def load_raw(name, w, c0, width):
+            raw = held.tile([P, PACK, width], F32, name=name)
+            nc.sync.dma_start(raw[:], w.rearrange("(p j) n -> p j n", j=PACK)[:, :, c0 : c0 + width])
+            return raw
+
         offsets = held.tile([P, J // 16], U16, name="offsets")
         nc.sync.dma_start(offsets[:], offs)
-        bias_rows = held.tile([P, P], F32, name="bias_rows", tag="v2_slot")
+        wi_raw_a = load_raw("wi_raw_a", wi, 0, NH)
+
+        bias_rows = held.tile([P, P], F32, name="bias_rows")
         nc.gpsimd.memset(bias_rows[:], 0.0)
-        nc.scalar.dma_start(bias_rows[0:4, :], br.rearrange("(c p) -> c p", p=P))
-        nc.scalar.dma_start(bias_rows[4:8, :], bi.rearrange("(c p) -> c p", p=P))
-        identity = held.tile([P, P], F32, name="identity", tag="v_slot")
-        make_identity(nc, identity[:])
+        w4_scales = held.tile([P, N], U8, name="w4_scales", align_bytes=64)
+        nc.gpsimd.memset(w4_scales[:].bitcast(I32), 0)
+        nc.gpsimd.dma_start(bias_rows[0:4, :], br.rearrange("(c p) -> c p", p=P))
+        nc.gpsimd.dma_start(bias_rows[4:8, :], bi.rearrange("(c p) -> c p", p=P))
+        for q in range(4):
+            nc.sync.dma_start(
+                w4_scales[32 * q : 32 * q + 4, :].bitcast(I32), wr4_scales[0, 4 * q : 4 * q + 4, :].bitcast(I32)
+            )
 
         def load_scale_window(name, scales):
-            window = held.tile([P, T // 4], I32, name=name)
+            window = held.tile([P, T // 4], I32, name=name, tag=name, align_bytes=64)
             nc.vector.memset(window[:], 0)
-            nc.scalar.dma_start(window[0:P:8, :], scales[0].bitcast(I32))
+            nc.sync.dma_start(window[0:P:8, :], scales[0].bitcast(I32))
             return window
 
         s2_window = load_scale_window("s2_window", tab2_scales)
         s_window = load_scale_window("s_window", tab_scales)
-
+        v2_window = held.tile([P, T], I32, name="v2_window", tag="v2_window", align_bytes=64)
+        nc.sync.dma_start(v2_window[:], words_ap(tab2_words))
         w4_codes = held.tile([P, 2 * N], U8, name="w4_codes", align_bytes=64)
         nc.sync.dma_start(w4_codes[:].bitcast(I32), wr4_words[0].bitcast(I32))
 
-        def load_raw(name, w, c0, width):
-            raw = raws.tile([P, PACK, width], F32, name=name, tag="raw")
-            nc.sync.dma_start(raw[:], w.rearrange("(p j) n -> p j n", j=PACK)[:, :, c0 : c0 + width])
-            return raw
-
-        wrd_raw = load_raw("wrd_raw", wrd, 0, N)
-        wi_raw_a = load_raw("wi_raw_a", wi, 0, NH)
-
-        w4_scales = held.tile([P, N], U8, name="w4_scales", align_bytes=64)
-        nc.gpsimd.memset(w4_scales[:], 0)
-        for q in range(4):
-            nc.gpsimd.dma_start(
-                w4_scales[32 * q : 32 * q + 4, :].bitcast(I32), wr4_scales[0, 4 * q : 4 * q + 4, :].bitcast(I32)
-            )
+        identity = held.tile([P, P], F32, name="identity")
+        make_identity(nc, identity[:])
         bias_bank = psum.tile([P, JH], F32, name="bias_bank", tag="bank")
         nc.tensor.transpose(bias_bank[:, 0:P], bias_rows[:], identity[:])
         bias = held.tile([P, 8], F32, name="bias")
         nc.scalar.activation(bias[:], bias_bank[:, 0:8], IDENTITY)
-        v2_window = held.tile([P, T], I32, name="v2_window", tag="v2_slot")
-        nc.sync.dma_start(v2_window[:], words_ap(tab2_words))
-        v_window = held.tile([P, T], I32, name="v_window", tag="v_slot")
-        nc.sync.dma_start(v_window[:], words_ap(tab_words))
 
         def gather_scales(name, window):
+            plane = held.tile([P, J], U8, name=name + "_plane", align_bytes=64)
+            nc.vector.memset(plane[:].bitcast(I32), 0)
             picked = held.tile([P, J], U8, name=name + "_picked", align_bytes=64)
             nc.vector.tensor_copy(picked[:], window[:].bitcast(U8).indirect(offsets[:]))
-            plane = held.tile([P, J], U8, name=name + "_plane", align_bytes=64)
-            nc.vector.tensor_copy(plane[:].bitcast(I32), picked[:].bitcast(I32))
-            for r in range(1, 4):
-                nc.scalar.dma_start(plane[r:P:32, :].bitcast(I32), picked[8 * r : P : 32, :].bitcast(I32))
+            for q in range(4):
+                nc.sync.dma_start(
+                    plane[32 * q : 32 * q + 4, :].bitcast(I32), picked[32 * q : 32 * (q + 1) : 8, :].bitcast(I32)
+                )
             return plane
 
         def gather_words(name, window, h):
@@ -97,7 +94,11 @@ def tile_list_cpxtab_dl_bias_kernel(
             return picked
 
         s2_plane = gather_scales("s2", s2_window)
+        wrd_raw = load_raw("wrd_raw", wrd, 0, N)
         s_plane = gather_scales("s", s_window)
+        v_window = held.tile([P, T], I32, name="v_window")
+        nc.sync.dma_start(v_window[:], words_ap(tab_words))
+        wi_raw_b = load_raw("wi_raw_b", wi, NH, NH)
         v2_codes = [gather_words("v2_codes", v2_window, h) for h in range(2)]
 
         def new_weight(name):
@@ -118,16 +119,16 @@ def tile_list_cpxtab_dl_bias_kernel(
                 in_=grouped[:].rearrange("p n j -> p (n j)"),
             )
 
-        def interleave(name, raw_cols, on_scalar):
-            grouped = held.tile([P, NH, PACK], BF16, name=name, align_bytes=64)
+        def interleave(name, raw_cols, on_scalar, tag):
+            grouped = held.tile([P, NH, PACK], BF16, name=name, align_bytes=64, tag=tag)
             if on_scalar:
                 nc.scalar.copy(grouped[:], raw_cols.rearrange("p j n -> p n j"))
             else:
                 nc.vector.tensor_copy(grouped[:], raw_cols.rearrange("p j n -> p n j"))
             return grouped
 
-        def negate(name, grouped):
-            negated = held.tile([P, NH, PACK], BF16, name=name, align_bytes=64)
+        def negate(name, grouped, tag):
+            negated = held.tile([P, NH, PACK], BF16, name=name, align_bytes=64, tag=tag)
             nc.vector.tensor_scalar(negated[:], grouped[:], -1.0, None, MULT)
             return negated
 
@@ -148,56 +149,75 @@ def tile_list_cpxtab_dl_bias_kernel(
                 stop=stop,
             )
 
-        zi_banks = {}
-        for h in range(2):
-            for n in range(4):
-                zi_banks[n, h] = psum.tile([P, JH], F32, name="zi_%d_%d" % (n, h), tag="bank")
-                mx_pass(zi_banks[n, h], None, n, v2_codes, s2_plane, h, True, False)
-        for a in range(2):
-            quantize(wrd_q, NH * a, interleave("wrd_g%d" % a, wrd_raw[:, :, NH * a : NH * (a + 1)], True))
-            for n in (2 * a, 2 * a + 1):
-                for h in range(2):
-                    mx_pass(zi_banks[n, h], wrd_q, n, v2_codes, s2_plane, h, False, False)
-        wi_raw_b = load_raw("wi_raw_b", wi, NH, NH)
-        wi_g = interleave("wi_g0", wi_raw_a[:], True)
-        neg_g = negate("neg_g0", wi_g)
-        quantize(wi_q, 0, wi_g)
-        quantize(neg_q, 0, neg_g)
-
-        v_codes = [gather_words("v_codes", v_window, h) for h in range(2)]
-        wi_g = interleave("wi_g1", wi_raw_b[:], False)
-        neg_g = negate("neg_g1", wi_g)
-        quantize(wi_q, NH, wi_g)
-        quantize(neg_q, NH, neg_g)
-
         results = {}
         for part in range(2):
             for n in range(4):
                 results[part, n] = held.tile([P, J], F32, name="result_%d_%d" % (part, n))
         outs = (out_0, out_1)
+        banks = {}
+        partial = {}
 
-        order = [(1, 0, 0), (1, 1, 0), (0, 0, 0), (1, 0, 1), (1, 1, 1), (0, 0, 1)]
-        order += [(1, n, h) for n in (2, 3) for h in range(2)]
-        order += [(0, n, h) for n in (1, 2, 3) for h in range(2)]
-        paired = [(1, 2), (1, 3), (0, 1), (0, 2)]
-        for i, (part, n, h) in enumerate(order):
-            if part == 1:
-                bank = zi_banks[n, h]
-                mx_pass(bank, wi_q, n, v_codes, s_plane, h, False, True)
+        def open_bank(part, n, h, name):
+            banks[part, n, h] = psum.tile([P, JH], F32, name="%s_%d_%d" % (name, n, h), tag="bank")
+            return banks[part, n, h]
+
+        def add_bias(out, part, n, h, on_scalar):
+            column = bias[:, 4 * part + n : 4 * part + n + 1]
+            if on_scalar:
+                nc.scalar.activation(out, banks[part, n, h][:], IDENTITY, bias=column)
             else:
-                bank = psum.tile([P, JH], F32, name="zr_%d_%d" % (n, h), tag="bank")
-                mx_pass(bank, neg_q, n, v2_codes, s2_plane, h, True, False)
-                mx_pass(bank, None, n, v_codes, s_plane, h, False, False)
-                mx_pass(bank, wrd_q, n, v_codes, s_plane, h, False, True)
+                nc.vector.tensor_scalar(out, banks[part, n, h][:], column, None, ADD)
+
+        wi_g = interleave("wi_g0", wi_raw_a[:], True, "s2_window")
+        quantize(wi_q, 0, wi_g)
+        for h in range(2):
+            for n in (2, 3, 0, 1):
+                mx_pass(open_bank(1, n, h, "zi"), None, n, v2_codes, s2_plane, h, True, False)
+        wrd_g = [
+            interleave("wrd_g%d" % a, wrd_raw[:, :, NH * a : NH * (a + 1)], a == 0, "wrd_g%d" % a) for a in range(2)
+        ]
+        neg_g = negate("neg_g0", wi_g, "v2_window")
+        quantize(wrd_q, NH, wrd_g[1])
+        quantize(neg_q, 0, neg_g)
+        quantize(wrd_q, 0, wrd_g[0])
+        for h in range(2):
+            for n in (2, 3):
+                mx_pass(banks[1, n, h], wrd_q, n, v2_codes, s2_plane, h, False, True)
+                partial[n, h] = held.tile([P, JH], F32, name="partial_%d_%d" % (n, h))
+                add_bias(partial[n, h][:], 1, n, h, n == 3)
+        for h in range(2):
+            for n in (0, 1):
+                mx_pass(banks[1, n, h], wrd_q, n, v2_codes, s2_plane, h, False, False)
+        for h in range(2):
+            for n in (0, 1):
+                mx_pass(open_bank(0, n, h, "zr"), neg_q, n, v2_codes, s2_plane, h, True, False)
+
+        v_codes = [gather_words("v_codes", v_window, h) for h in range(2)]
+        wi_g = interleave("wi_g1", wi_raw_b[:], False, "wi_g1")
+        neg_g = negate("neg_g1", wi_g, "neg_g1")
+        quantize(wi_q, NH, wi_g)
+        quantize(neg_q, NH, neg_g)
+
+        order = [(part, n, h) for h in range(2) for part in (1, 0) for n in (0, 1)]
+        order += [(1, 2, 0), (1, 2, 1), (0, 2, 0), (1, 3, 0), (0, 2, 1), (1, 3, 1), (0, 3, 0), (0, 3, 1)]
+        for part, n, h in order:
             cols = slice(JH * h, JH * (h + 1))
             result = results[part, n]
-            column = bias[:, 4 * part + n : 4 * part + n + 1]
-            if i >= 5 and i % 2 == 1:
-                nc.vector.tensor_scalar(result[:, cols], bank[:], column, None, ADD)
+            if part == 1 and n < 2:
+                mx_pass(banks[part, n, h], wi_q, n, v_codes, s_plane, h, False, True)
+                add_bias(result[:, cols], part, n, h, True)
+            elif part == 1:
+                bank = open_bank(part, n, h, "zi_rest")
+                mx_pass(bank, wi_q, n, v_codes, s_plane, h, True, True)
+                nc.vector.tensor_tensor(result[:, cols], bank[:], partial[n, h][:], ADD)
             else:
-                nc.scalar.activation(result[:, cols], bank[:], IDENTITY, bias=column)
+                if n >= 2:
+                    mx_pass(open_bank(part, n, h, "zr"), neg_q, n, v2_codes, s2_plane, h, True, False)
+                mx_pass(banks[part, n, h], None, n, v_codes, s_plane, h, False, False)
+                mx_pass(banks[part, n, h], wrd_q, n, v_codes, s_plane, h, False, True)
+                add_bias(result[:, cols], part, n, h, (n, h) not in ((1, 1), (3, 1)))
             rows = slice(M * n, M * (n + 1))
-            if (part, n) not in paired:
+            if n < 2 or (part, n) == (0, 3):
                 nc.sync.dma_start(outs[part][rows, cols], result[:, cols])
             elif h == 1:
                 nc.sync.dma_start(outs[part][rows, :], result[:])

@@ -23,6 +23,14 @@ PACK = 4
 M = 128
 JH = 512
 NH = 256
+RAW_BYTES = 4 * PACK * NH
+BIAS_AT = RAW_BYTES
+V_AT = BIAS_AT + 4 * P
+S2_AT = RAW_BYTES // 2
+WRD_B_AT = V_AT + 4 * T
+WRD_CODES_AT = WRD_B_AT + RAW_BYTES
+WI_B_AT = WRD_CODES_AT + 4 * N
+S_AT = WRD_CODES_AT - 4 * P
 
 
 def tile_list_cpxtab_dl_bias_kernel(
@@ -31,50 +39,46 @@ def tile_list_cpxtab_dl_bias_kernel(
     nc = tc.nc
     with ExitStack() as ctx:
         held = ctx.enter_context(tc.tile_pool(name="held", bufs=1))
+        placed = ctx.enter_context(tc.tile_pool(name="placed", bufs=1))
         psum = ctx.enter_context(tc.psum_pool(name="psum", bufs=8))
 
         def words_ap(words):
             return words[0].rearrange("p t i -> p (t i)").bitcast(I32)
 
-        def load_raw(name, w, c0, width):
-            raw = held.tile([P, PACK, width], F32, name=name)
-            nc.sync.dma_start(raw[:], w.rearrange("(p j) n -> p j n", j=PACK)[:, :, c0 : c0 + width])
-            return raw
+        def load_raw(raw, w, c0):
+            nc.sync.dma_start(raw[:], w.rearrange("(p j) n -> p j n", j=PACK)[:, :, c0 : c0 + NH])
+
+        def placed_raw(name, offset):
+            return placed.tile([P, PACK, NH], F32, name=name, offset=offset)
 
         offsets = held.tile([P, J // 16], U16, name="offsets")
         nc.sync.dma_start(offsets[:], offs)
-        wi_raw_a = load_raw("wi_raw_a", wi, 0, NH)
+        wrd_raw_a = held.tile([P, PACK, NH], F32, name="wrd_raw_a")
+        load_raw(wrd_raw_a, wrd, 0)
 
-        bias_rows = held.tile([P, P], F32, name="bias_rows")
-        nc.gpsimd.memset(bias_rows[:], 0.0)
         w4_scales = held.tile([P, N], U8, name="w4_scales", align_bytes=64)
         nc.gpsimd.memset(w4_scales[:].bitcast(I32), 0)
-        nc.gpsimd.dma_start(bias_rows[0:4, :], br.rearrange("(c p) -> c p", p=P))
-        nc.gpsimd.dma_start(bias_rows[4:8, :], bi.rearrange("(c p) -> c p", p=P))
         for q in range(4):
             nc.sync.dma_start(
                 w4_scales[32 * q : 32 * q + 4, :].bitcast(I32), wr4_scales[0, 4 * q : 4 * q + 4, :].bitcast(I32)
             )
 
-        def load_scale_window(name, scales):
-            window = held.tile([P, T // 4], I32, name=name, tag=name, align_bytes=64)
+        def load_scale_window(name, scales, offset):
+            window = placed.tile([P, T // 4], I32, name=name, offset=offset)
             nc.vector.memset(window[:], 0)
             nc.sync.dma_start(window[0:P:8, :], scales[0].bitcast(I32))
             return window
 
-        s2_window = load_scale_window("s2_window", tab2_scales)
-        s_window = load_scale_window("s_window", tab_scales)
-        v2_window = held.tile([P, T], I32, name="v2_window", tag="v2_window", align_bytes=64)
+        s2_window = load_scale_window("s2_window", tab2_scales, S2_AT)
+        v2_window = held.tile([P, T], I32, name="v2_window")
         nc.sync.dma_start(v2_window[:], words_ap(tab2_words))
+        s_window = load_scale_window("s_window", tab_scales, S_AT)
         w4_codes = held.tile([P, 2 * N], U8, name="w4_codes", align_bytes=64)
         nc.sync.dma_start(w4_codes[:].bitcast(I32), wr4_words[0].bitcast(I32))
 
         identity = held.tile([P, P], F32, name="identity")
         make_identity(nc, identity[:])
-        bias_bank = psum.tile([P, JH], F32, name="bias_bank", tag="bank")
-        nc.tensor.transpose(bias_bank[:, 0:P], bias_rows[:], identity[:])
         bias = held.tile([P, 8], F32, name="bias")
-        nc.scalar.activation(bias[:], bias_bank[:, 0:8], IDENTITY)
 
         def gather_scales(name, window):
             plane = held.tile([P, J], U8, name=name + "_plane", align_bytes=64)
@@ -94,12 +98,20 @@ def tile_list_cpxtab_dl_bias_kernel(
             return picked
 
         s2_plane = gather_scales("s2", s2_window)
-        wrd_raw = load_raw("wrd_raw", wrd, 0, N)
-        s_plane = gather_scales("s", s_window)
-        v_window = held.tile([P, T], I32, name="v_window")
+        wi_raw_a = placed_raw("wi_raw_a", 0)
+        load_raw(wi_raw_a, wi, 0)
+        bias_rows = placed.tile([P, P], F32, name="bias_rows", offset=BIAS_AT)
+        nc.gpsimd.memset(bias_rows[:], 0.0)
+        nc.sync.dma_start(bias_rows[0:4, :], br.rearrange("(c p) -> c p", p=P))
+        nc.sync.dma_start(bias_rows[4:8, :], bi.rearrange("(c p) -> c p", p=P))
+        v_window = placed.tile([P, T], I32, name="v_window", offset=V_AT)
         nc.sync.dma_start(v_window[:], words_ap(tab_words))
-        wi_raw_b = load_raw("wi_raw_b", wi, NH, NH)
         v2_codes = [gather_words("v2_codes", v2_window, h) for h in range(2)]
+        s_plane = gather_scales("s", s_window)
+        wrd_raw_b = placed_raw("wrd_raw_b", WRD_B_AT)
+        load_raw(wrd_raw_b, wrd, NH)
+        wi_raw_b = placed_raw("wi_raw_b", WI_B_AT)
+        load_raw(wi_raw_b, wi, NH)
 
         def new_weight(name):
             return (
@@ -107,7 +119,10 @@ def tile_list_cpxtab_dl_bias_kernel(
                 held.tile([P, N], U8, name=name + "_scales", align_bytes=64),
             )
 
-        wrd_q = new_weight("wrd")
+        wrd_q = (
+            placed.tile([P, N], U32, name="wrd_codes", align_bytes=64, offset=WRD_CODES_AT),
+            held.tile([P, N], U8, name="wrd_scales", align_bytes=64),
+        )
         wi_q = new_weight("wi")
         neg_q = new_weight("neg_wi")
 
@@ -119,16 +134,16 @@ def tile_list_cpxtab_dl_bias_kernel(
                 in_=grouped[:].rearrange("p n j -> p (n j)"),
             )
 
-        def interleave(name, raw_cols, on_scalar, tag):
-            grouped = held.tile([P, NH, PACK], BF16, name=name, align_bytes=64, tag=tag)
+        def interleave(name, raw_cols, on_scalar):
+            grouped = held.tile([P, NH, PACK], BF16, name=name, align_bytes=64)
             if on_scalar:
                 nc.scalar.copy(grouped[:], raw_cols.rearrange("p j n -> p n j"))
             else:
                 nc.vector.tensor_copy(grouped[:], raw_cols.rearrange("p j n -> p n j"))
             return grouped
 
-        def negate(name, grouped, tag):
-            negated = held.tile([P, NH, PACK], BF16, name=name, align_bytes=64, tag=tag)
+        def negate(name, grouped):
+            negated = held.tile([P, NH, PACK], BF16, name=name, align_bytes=64)
             nc.vector.tensor_scalar(negated[:], grouped[:], -1.0, None, MULT)
             return negated
 
@@ -168,23 +183,21 @@ def tile_list_cpxtab_dl_bias_kernel(
             else:
                 nc.vector.tensor_scalar(out, banks[part, n, h][:], column, None, ADD)
 
-        wi_g = interleave("wi_g0", wi_raw_a[:], True, "s2_window")
-        quantize(wi_q, 0, wi_g)
-        for h in range(2):
-            for n in (2, 3, 0, 1):
-                mx_pass(open_bank(1, n, h, "zi"), None, n, v2_codes, s2_plane, h, True, False)
-        wrd_g = [
-            interleave("wrd_g%d" % a, wrd_raw[:, :, NH * a : NH * (a + 1)], a == 0, "wrd_g%d" % a) for a in range(2)
-        ]
-        neg_g = negate("neg_g0", wi_g, "v2_window")
-        quantize(wrd_q, NH, wrd_g[1])
-        quantize(neg_q, 0, neg_g)
-        quantize(wrd_q, 0, wrd_g[0])
+        quantize(wrd_q, 0, interleave("wrd_g0", wrd_raw_a[:], True))
+        wi_g = interleave("wi_g0", wi_raw_a[:], True)
         for h in range(2):
             for n in (2, 3):
-                mx_pass(banks[1, n, h], wrd_q, n, v2_codes, s2_plane, h, False, True)
+                mx_pass(open_bank(1, n, h, "zi_base"), None, n, v2_codes, s2_plane, h, True, True)
                 partial[n, h] = held.tile([P, JH], F32, name="partial_%d_%d" % (n, h))
-                add_bias(partial[n, h][:], 1, n, h, n == 3)
+                nc.scalar.copy(partial[n, h][:], banks[1, n, h][:])
+            for n in (0, 1):
+                mx_pass(open_bank(1, n, h, "zi"), None, n, v2_codes, s2_plane, h, True, False)
+        bias_bank = psum.tile([P, JH], F32, name="bias_bank", tag="bank")
+        nc.tensor.transpose(bias_bank[:, 0:P], bias_rows[:], identity[:])
+        nc.scalar.activation(bias[:], bias_bank[:, 0:8], IDENTITY)
+        neg_g = negate("neg_g0", wi_g)
+        quantize(wi_q, 0, wi_g)
+        quantize(neg_q, 0, neg_g)
         for h in range(2):
             for n in (0, 1):
                 mx_pass(banks[1, n, h], wrd_q, n, v2_codes, s2_plane, h, False, False)
@@ -193,31 +206,56 @@ def tile_list_cpxtab_dl_bias_kernel(
                 mx_pass(open_bank(0, n, h, "zr"), neg_q, n, v2_codes, s2_plane, h, True, False)
 
         v_codes = [gather_words("v_codes", v_window, h) for h in range(2)]
-        wi_g = interleave("wi_g1", wi_raw_b[:], False, "wi_g1")
-        neg_g = negate("neg_g1", wi_g, "neg_g1")
+        wrd_g = interleave("wrd_g1", wrd_raw_b[:], False)
+        wi_g = interleave("wi_g1", wi_raw_b[:], False)
+        quantize(wrd_q, NH, wrd_g)
+        neg_g = negate("neg_g1", wi_g)
         quantize(wi_q, NH, wi_g)
         quantize(neg_q, NH, neg_g)
 
-        order = [(part, n, h) for h in range(2) for part in (1, 0) for n in (0, 1)]
-        order += [(1, 2, 0), (1, 2, 1), (0, 2, 0), (1, 3, 0), (0, 2, 1), (1, 3, 1), (0, 3, 0), (0, 3, 1)]
-        for part, n, h in order:
+        def finish(part, n, h):
             cols = slice(JH * h, JH * (h + 1))
             result = results[part, n]
-            if part == 1 and n < 2:
-                mx_pass(banks[part, n, h], wi_q, n, v_codes, s_plane, h, False, True)
-                add_bias(result[:, cols], part, n, h, True)
-            elif part == 1:
-                bank = open_bank(part, n, h, "zi_rest")
-                mx_pass(bank, wi_q, n, v_codes, s_plane, h, True, True)
-                nc.vector.tensor_tensor(result[:, cols], bank[:], partial[n, h][:], ADD)
+            if part == 1 and n >= 2:
+                column = bias[:, 4 * part + n : 4 * part + n + 1]
+                nc.vector.scalar_tensor_tensor(
+                    result[:, cols], banks[part, n, h][:], column, partial[n, h][:], ADD, ADD
+                )
             else:
-                if n >= 2:
-                    mx_pass(open_bank(part, n, h, "zr"), neg_q, n, v2_codes, s2_plane, h, True, False)
-                mx_pass(banks[part, n, h], None, n, v_codes, s_plane, h, False, False)
-                mx_pass(banks[part, n, h], wrd_q, n, v_codes, s_plane, h, False, True)
-                add_bias(result[:, cols], part, n, h, (n, h) not in ((1, 1), (3, 1)))
+                add_bias(result[:, cols], part, n, h, (n, h) != (3, 1))
             rows = slice(M * n, M * (n + 1))
             if n < 2 or (part, n) == (0, 3):
                 nc.sync.dma_start(outs[part][rows, cols], result[:, cols])
             elif h == 1:
                 nc.sync.dma_start(outs[part][rows, :], result[:])
+
+        def wr_times_v(n, h, start, stop):
+            mx_pass(banks[0, n, h], None, n, v_codes, s_plane, h, start, False)
+            mx_pass(banks[0, n, h], wrd_q, n, v_codes, s_plane, h, False, stop)
+
+        for h in range(2):
+            for n in (0, 1):
+                mx_pass(banks[1, n, h], wi_q, n, v_codes, s_plane, h, False, True)
+                finish(1, n, h)
+            for n in (0, 1):
+                wr_times_v(n, h, False, True)
+                finish(0, n, h)
+        for h in range(2):
+            open_bank(0, 2, h, "zr")
+            wr_times_v(2, h, True, False)
+        for h in range(2):
+            mx_pass(open_bank(1, 2, h, "zi"), wrd_q, 2, v2_codes, s2_plane, h, True, False)
+        for h in range(2):
+            mx_pass(banks[1, 2, h], wi_q, 2, v_codes, s_plane, h, False, True)
+            finish(1, 2, h)
+        for h in range(2):
+            mx_pass(banks[0, 2, h], neg_q, 2, v2_codes, s2_plane, h, False, True)
+            finish(0, 2, h)
+        for h in range(2):
+            mx_pass(open_bank(1, 3, h, "zi"), wrd_q, 3, v2_codes, s2_plane, h, True, False)
+            mx_pass(banks[1, 3, h], wi_q, 3, v_codes, s_plane, h, False, True)
+            finish(1, 3, h)
+        for h in range(2):
+            mx_pass(open_bank(0, 3, h, "zr"), neg_q, 3, v2_codes, s2_plane, h, True, False)
+            wr_times_v(3, h, False, True)
+            finish(0, 3, h)

@@ -24,9 +24,10 @@ M = 128
 JH = 512
 NH = 256
 RAW_BYTES = 4 * PACK * NH
-BIAS_AT = RAW_BYTES
-V_AT = BIAS_AT + 4 * P
-S2_AT = RAW_BYTES // 2
+S2_AT = 0
+BIAS_AT = 0
+IDENTITY_AT = BIAS_AT + 4 * P
+V_AT = IDENTITY_AT + 4 * P
 WRD_B_AT = V_AT + 4 * T
 WRD_CODES_AT = WRD_B_AT + RAW_BYTES
 WI_B_AT = WRD_CODES_AT + 4 * N
@@ -75,9 +76,9 @@ def tile_list_cpxtab_dl_bias_kernel(
         s_window = load_scale_window("s_window", tab_scales, S_AT)
         w4_codes = held.tile([P, 2 * N], U8, name="w4_codes", align_bytes=64)
         nc.sync.dma_start(w4_codes[:].bitcast(I32), wr4_words[0].bitcast(I32))
+        wi_raw_a = held.tile([P, PACK, NH], F32, name="wi_raw_a")
+        load_raw(wi_raw_a, wi, 0)
 
-        identity = held.tile([P, P], F32, name="identity")
-        make_identity(nc, identity[:])
         bias = held.tile([P, 8], F32, name="bias")
 
         def gather_scales(name, window):
@@ -98,12 +99,12 @@ def tile_list_cpxtab_dl_bias_kernel(
             return picked
 
         s2_plane = gather_scales("s2", s2_window)
-        wi_raw_a = placed_raw("wi_raw_a", 0)
-        load_raw(wi_raw_a, wi, 0)
         bias_rows = placed.tile([P, P], F32, name="bias_rows", offset=BIAS_AT)
         nc.gpsimd.memset(bias_rows[:], 0.0)
         nc.sync.dma_start(bias_rows[0:4, :], br.rearrange("(c p) -> c p", p=P))
         nc.sync.dma_start(bias_rows[4:8, :], bi.rearrange("(c p) -> c p", p=P))
+        identity = placed.tile([P, P], F32, name="identity", offset=IDENTITY_AT)
+        make_identity(nc, identity[:])
         v_window = placed.tile([P, T], I32, name="v_window", offset=V_AT)
         nc.sync.dma_start(v_window[:], words_ap(tab_words))
         v2_codes = [gather_words("v2_codes", v2_window, h) for h in range(2)]

from contextlib import ExitStack

import concourse.mybir as mybir
from concourse.masks import make_identity

K, N, T, J = 512, 512, 4096, 1024
FLOPS = 6 * 2 * K * N * J

F32 = mybir.dt.float32
BF16 = mybir.dt.bfloat16
I32 = mybir.dt.int32
U32 = mybir.dt.uint32
U16 = mybir.dt.uint16
U8 = mybir.dt.uint8
FP8X4 = mybir.dt.float8_e4m3fn_x4
FP4X4 = mybir.dt.float4_e2m1fn_x4
ADD = mybir.AluOpType.add
MULT = mybir.AluOpType.mult
IDENTITY = mybir.ActivationFunctionType.Identity

P = 128
PACK = 4
M = 128
JH = 512
NH = 256
RAW_BYTES = 4 * PACK * NH
S2_AT = 0
BIAS_AT = 0
IDENTITY_AT = BIAS_AT + 4 * P
V_AT = IDENTITY_AT + 4 * P
WRD_B_AT = V_AT + 4 * T
WRD_CODES_AT = WRD_B_AT + RAW_BYTES
WI_B_AT = WRD_CODES_AT + 4 * N
S_AT = WRD_CODES_AT - 4 * P


def tile_list_cpxtab_dl_bias_kernel(
    tc, tab_words, tab_scales, tab2_words, tab2_scales, wr4_words, wr4_scales, wrd, wi, br, bi, offs, out_0, out_1
):
    nc = tc.nc
    with ExitStack() as ctx:
        held = ctx.enter_context(tc.tile_pool(name="held", bufs=1))
        placed = ctx.enter_context(tc.tile_pool(name="placed", bufs=1))
        psum = ctx.enter_context(tc.psum_pool(name="psum", bufs=8))

        def words_ap(words):
            return words[0].rearrange("p t i -> p (t i)").bitcast(I32)

        def load_raw(raw, w, c0):
            nc.sync.dma_start(raw[:], w.rearrange("(p j) n -> p j n", j=PACK)[:, :, c0 : c0 + NH])

        def placed_raw(name, offset):
            return placed.tile([P, PACK, NH], F32, name=name, offset=offset)

        offsets = held.tile([P, J // 16], U16, name="offsets")
        nc.sync.dma_start(offsets[:], offs)
        wrd_raw_a = held.tile([P, PACK, NH], F32, name="wrd_raw_a")
        load_raw(wrd_raw_a, wrd, 0)

        w4_scales = held.tile([P, N], U8, name="w4_scales", align_bytes=64)
        nc.gpsimd.memset(w4_scales[:].bitcast(I32), 0)
        for q in range(4):
            nc.sync.dma_start(
                w4_scales[32 * q : 32 * q + 4, :].bitcast(I32), wr4_scales[0, 4 * q : 4 * q + 4, :].bitcast(I32)
            )

        def load_scale_window(name, scales, offset):
            window = placed.tile([P, T // 4], I32, name=name, offset=offset)
            nc.vector.memset(window[:], 0)
            nc.sync.dma_start(window[0:P:8, :], scales[0].bitcast(I32))
            return window

        s2_window = load_scale_window("s2_window", tab2_scales, S2_AT)
        v2_window = held.tile([P, T], I32, name="v2_window")
        nc.sync.dma_start(v2_window[:], words_ap(tab2_words))
        s_window = load_scale_window("s_window", tab_scales, S_AT)
        w4_codes = held.tile([P, 2 * N], U8, name="w4_codes", align_bytes=64)
        nc.sync.dma_start(w4_codes[:].bitcast(I32), wr4_words[0].bitcast(I32))
        wi_raw_a = held.tile([P, PACK, NH], F32, name="wi_raw_a")
        load_raw(wi_raw_a, wi, 0)

        bias = held.tile([P, 8], F32, name="bias")

        def gather_scales(name, window):
            plane = held.tile([P, J], U8, name=name + "_plane", align_bytes=64)
            nc.vector.memset(plane[:].bitcast(I32), 0)
            picked = held.tile([P, J], U8, name=name + "_picked", align_bytes=64)
            nc.vector.tensor_copy(picked[:], window[:].bitcast(U8).indirect(offsets[:]))
            for q in range(4):
                nc.sync.dma_start(
                    plane[32 * q : 32 * q + 4, :].bitcast(I32), picked[32 * q : 32 * (q + 1) : 8, :].bitcast(I32)
                )
            return plane

        def gather_words(name, window, h):
            picked = held.tile([P, JH], U32, name=name + "_%d" % h, align_bytes=64)
            cols = JH // 16
            nc.vector.tensor_copy(picked[:], window[:].bitcast(U32).indirect(offsets[:, h * cols : (h + 1) * cols]))
            return picked

        s2_plane = gather_scales("s2", s2_window)
        bias_rows = placed.tile([P, P], F32, name="bias_rows", offset=BIAS_AT)
        nc.gpsimd.memset(bias_rows[:], 0.0)
        nc.sync.dma_start(bias_rows[0:4, :], br.rearrange("(c p) -> c p", p=P))
        nc.sync.dma_start(bias_rows[4:8, :], bi.rearrange("(c p) -> c p", p=P))
        identity = placed.tile([P, P], F32, name="identity", offset=IDENTITY_AT)
        make_identity(nc, identity[:])
        v_window = placed.tile([P, T], I32, name="v_window", offset=V_AT)
        nc.sync.dma_start(v_window[:], words_ap(tab_words))
        v2_codes = [gather_words("v2_codes", v2_window, h) for h in range(2)]
        s_plane = gather_scales("s", s_window)
        wrd_raw_b = placed_raw("wrd_raw_b", WRD_B_AT)
        load_raw(wrd_raw_b, wrd, NH)
        wi_raw_b = placed_raw("wi_raw_b", WI_B_AT)
        load_raw(wi_raw_b, wi, NH)

        def new_weight(name):
            return (
                held.tile([P, N], U32, name=name + "_codes", align_bytes=64),
                held.tile([P, N], U8, name=name + "_scales", align_bytes=64),
            )

        wrd_q = (
            placed.tile([P, N], U32, name="wrd_codes", align_bytes=64, offset=WRD_CODES_AT),
            held.tile([P, N], U8, name="wrd_scales", align_bytes=64),
        )
        wi_q = new_weight("wi")
        neg_q = new_weight("neg_wi")

        def quantize(weight, c0, grouped):
            codes, scales = weight
            nc.vector.quantize_mx(
                out=codes[:, c0 : c0 + NH].bitcast(FP8X4),
                scales=scales[:, c0 : c0 + NH],
                in_=grouped[:].rearrange("p n j -> p (n j)"),
            )

        def interleave(name, raw_cols, on_scalar):
            grouped = held.tile([P, NH, PACK], BF16, name=name, align_bytes=64)
            if on_scalar:
                nc.scalar.copy(grouped[:], raw_cols.rearrange("p j n -> p n j"))
            else:
                nc.vector.tensor_copy(grouped[:], raw_cols.rearrange("p j n -> p n j"))
            return grouped

        def negate(name, grouped):
            negated = held.tile([P, NH, PACK], BF16, name=name, align_bytes=64)
            nc.vector.tensor_scalar(negated[:], grouped[:], -1.0, None, MULT)
            return negated

        def mx_pass(bank, weight, n, codes, plane, h, start, stop):
            if weight is None:
                lhs = w4_codes[:, 2 * M * n : 2 * M * (n + 1)].bitcast(FP4X4)
                lhs_scale = w4_scales[:, M * n : M * (n + 1)]
            else:
                lhs = weight[0][:, M * n : M * (n + 1)].bitcast(FP8X4)
                lhs_scale = weight[1][:, M * n : M * (n + 1)]
            nc.tensor.matmul_mx(
                out=bank[:],
                lhsT=lhs,
                lhsT_scale=lhs_scale,
                rhs=codes[h][:].bitcast(FP8X4),
                rhs_scale=plane[:, JH * h : JH * (h + 1)],
                start=start,
                stop=stop,
            )

        results = {}
        for part in range(2):
            for n in range(4):
                results[part, n] = held.tile([P, J], F32, name="result_%d_%d" % (part, n))
        outs = (out_0, out_1)
        banks = {}
        partial = {}

        def open_bank(part, n, h, name):
            banks[part, n, h] = psum.tile([P, JH], F32, name="%s_%d_%d" % (name, n, h), tag="bank")
            return banks[part, n, h]

        def add_bias(out, part, n, h, on_scalar):
            column = bias[:, 4 * part + n : 4 * part + n + 1]
            if on_scalar:
                nc.scalar.activation(out, banks[part, n, h][:], IDENTITY, bias=column)
            else:
                nc.vector.tensor_scalar(out, banks[part, n, h][:], column, None, ADD)

        quantize(wrd_q, 0, interleave("wrd_g0", wrd_raw_a[:], True))
        wi_g = interleave("wi_g0", wi_raw_a[:], True)
        for h in range(2):
            for n in (2, 3):
                mx_pass(open_bank(1, n, h, "zi_base"), None, n, v2_codes, s2_plane, h, True, True)
                partial[n, h] = held.tile([P, JH], F32, name="partial_%d_%d" % (n, h))
                nc.scalar.copy(partial[n, h][:], banks[1, n, h][:])
            for n in (0, 1):
                mx_pass(open_bank(1, n, h, "zi"), None, n, v2_codes, s2_plane, h, True, False)
        bias_bank = psum.tile([P, JH], F32, name="bias_bank", tag="bank")
        nc.tensor.transpose(bias_bank[:, 0:P], bias_rows[:], identity[:])
        nc.scalar.activation(bias[:], bias_bank[:, 0:8], IDENTITY)
        neg_g = negate("neg_g0", wi_g)
        quantize(wi_q, 0, wi_g)
        quantize(neg_q, 0, neg_g)
        for h in range(2):
            for n in (0, 1):
                mx_pass(banks[1, n, h], wrd_q, n, v2_codes, s2_plane, h, False, False)
        for h in range(2):
            for n in (0, 1):
                mx_pass(open_bank(0, n, h, "zr"), neg_q, n, v2_codes, s2_plane, h, True, False)

        v_codes = [gather_words("v_codes", v_window, h) for h in range(2)]
        wrd_g = interleave("wrd_g1", wrd_raw_b[:], False)
        wi_g = interleave("wi_g1", wi_raw_b[:], False)
        quantize(wrd_q, NH, wrd_g)
        neg_g = negate("neg_g1", wi_g)
        quantize(wi_q, NH, wi_g)
        quantize(neg_q, NH, neg_g)

        def finish(part, n, h):
            cols = slice(JH * h, JH * (h + 1))
            result = results[part, n]
            if part == 1 and n >= 2:
                column = bias[:, 4 * part + n : 4 * part + n + 1]
                nc.vector.scalar_tensor_tensor(
                    result[:, cols], banks[part, n, h][:], column, partial[n, h][:], ADD, ADD
                )
            else:
                add_bias(result[:, cols], part, n, h, (n, h) != (3, 1))
            rows = slice(M * n, M * (n + 1))
            if n < 2 or (part, n) == (0, 3):
                nc.sync.dma_start(outs[part][rows, cols], result[:, cols])
            elif h == 1:
                nc.sync.dma_start(outs[part][rows, :], result[:])

        def wr_times_v(n, h, start, stop):
            mx_pass(banks[0, n, h], None, n, v_codes, s_plane, h, start, False)
            mx_pass(banks[0, n, h], wrd_q, n, v_codes, s_plane, h, False, stop)

        for h in range(2):
            for n in (0, 1):
                mx_pass(banks[1, n, h], wi_q, n, v_codes, s_plane, h, False, True)
                finish(1, n, h)
            for n in (0, 1):
                wr_times_v(n, h, False, True)
                finish(0, n, h)
        for h in range(2):
            open_bank(0, 2, h, "zr")
            wr_times_v(2, h, True, False)
        for h in range(2):
            mx_pass(open_bank(1, 2, h, "zi"), wrd_q, 2, v2_codes, s2_plane, h, True, False)
        for h in range(2):
            mx_pass(banks[1, 2, h], wi_q, 2, v_codes, s_plane, h, False, True)
            finish(1, 2, h)
        for h in range(2):
            mx_pass(banks[0, 2, h], neg_q, 2, v2_codes, s2_plane, h, False, True)
            finish(0, 2, h)
        for h in range(2):
            mx_pass(open_bank(1, 3, h, "zi"), wrd_q, 3, v2_codes, s2_plane, h, True, False)
            mx_pass(banks[1, 3, h], wi_q, 3, v_codes, s_plane, h, False, True)
            finish(1, 3, h)
        for h in range(2):
            mx_pass(open_bank(0, 3, h, "zr"), neg_q, 3, v2_codes, s2_plane, h, True, False)
            wr_times_v(3, h, False, True)
            finish(0, 3, h)
